import numpy as np
import ml_dtypes


def mxq(x, axis, fmt="e4m3"):
    dtype, down = {"e4m3": (ml_dtypes.float8_e4m3fn, 7), "e5m2": (ml_dtypes.float8_e5m2, 14)}[fmt]
    v = np.moveaxis(np.asarray(x, np.float32).astype(ml_dtypes.bfloat16).astype(np.float64), axis, -1)
    blocks = v.reshape(v.shape[:-1] + (-1, 32))
    amax = np.abs(blocks).max(-1, keepdims=True)
    byte = np.maximum(np.where(amax > 0, np.frexp(amax)[1] - 1 + 127, 0) - down, 1)
    scale = np.exp2(byte - 127.0)
    codes = (blocks / scale).astype(np.float32).astype(dtype).astype(np.float64)
    return np.moveaxis((codes * scale).reshape(v.shape), -1, axis)


WIDE = False


def mx_kscale(k):
    if not WIDE:
        return np.ones(k)
    levels = np.array([10, -10, 5, -5, 0])
    if k % 512:
        return np.exp2(np.random.permutation(np.resize(levels, k // 32))).repeat(32)
    a = np.empty((k // 512, 16))
    for p in range(k // 512):
        a[p, :8] = np.random.permutation(np.resize(levels, 8))
        for g in range(8):
            far = levels[np.abs(levels - a[p, g]) >= 10]
            a[p, g + 8] = far[np.random.randint(len(far))]
    return np.exp2(a.ravel()).repeat(32)


def f64(x):
    return np.asarray(x).astype(np.float64)


def striped(idx):
    return np.tile(np.asarray(idx).reshape(-1, 16).T, (8, 1)).astype(np.uint16)


def unstriped(offs):
    return offs[:16].T.reshape(-1).astype(np.int64)


E2M1 = np.array([0.0, 0.5, 1.0, 1.5, 2.0, 3.0, 4.0, 6.0, -0.0, -0.5, -1.0, -1.5, -2.0, -3.0, -4.0, -6.0])


def pack_weight(w, fmt):
    k, n = w.shape
    w = f64(np.asarray(w, np.float32).astype(ml_dtypes.bfloat16)).reshape(k // 32, 32, n)
    amax = np.abs(w).max(1)
    if fmt == "e4m3":
        byte = np.frexp(amax)[1] - 1 + 127 - 7
    else:
        mant, ex = np.frexp(amax / 6.0)
        byte = np.where(mant > 0.5, ex, ex - 1) + 127
    byte = np.clip(np.where(amax > 0, byte, 1), 1, 254)
    scaled = (w * np.exp2(127.0 - byte)[:, None, :]).reshape(k, n).astype(np.float32)
    by_word = np.ascontiguousarray(scaled.reshape(k // 512, 128, 4, n).transpose(0, 1, 3, 2))
    if fmt == "e4m3":
        words = by_word.astype(ml_dtypes.float8_e4m3fn).view(np.uint8)
    else:
        c = by_word.astype(ml_dtypes.float4_e2m1fn).view(np.uint8) & 0xF
        words = (c[..., 0::2] | (c[..., 1::2] << 4)).reshape(k // 512, 128, 2 * n)
    return np.ascontiguousarray(words), np.ascontiguousarray(byte.astype(np.uint8).reshape(k // 512, 16, n))


def unpack_weight(words, scales, fmt):
    g, _, n = scales.shape
    words = np.ascontiguousarray(words).reshape(g, 128, n, -1)
    if fmt == "e4m3":
        vals = words.view(ml_dtypes.float8_e4m3fn).astype(np.float64)
    else:
        nib = np.empty((g, 128, n, 4), np.uint8)
        nib[..., 0::2] = words & 0xF
        nib[..., 1::2] = words >> 4
        vals = E2M1[nib]
    vals = vals * np.repeat(np.exp2(scales.astype(np.float64) - 127.0), 8, axis=1)[..., None]
    return vals.transpose(0, 1, 3, 2).reshape(g * 512, n)


def softplus(v):
    return np.log(1.0 + np.exp(v))


def sigmoid(v):
    return 1.0 / (1.0 + np.exp(-v))


K, R, F, T, J, M = 512, 128, 512, 2048, 512, 256


def setup_inputs():
    n = np.random.standard_normal
    idx = np.random.permutation(T)[:J]
    idx2 = np.random.permutation(J)[:M]
    idx3 = np.random.permutation(J)[:M]
    fk = mx_kscale(K)
    tabp = pack_weight(n((K, T)) / fk[:, None], "e4m3")
    dtabp = pack_weight(n((K, T)) / fk[:, None], "e4m3")
    return {
        "tab_words": tabp[0],
        "tab_scales": tabp[1],
        "dtab_words": dtabp[0],
        "dtab_scales": dtabp[1],
        "w1": (n((K, R)) * 1 / np.sqrt(K) * fk[:, None]).astype(np.float32),
        "bias": (np.random.uniform(-0.5, 0.5, (R, 1))).astype(np.float32),
        "reserve": (np.random.uniform(0.3, 1.0, (R, 1))).astype(np.float32),
        "og": (np.random.uniform(0.5, 2.0, (R, 1))).astype(np.float32),
        "base": (0.3 * n((R, M))).astype(np.float32),
        "offs": striped(idx),
        "offs2": striped(idx2),
        "offs3": striped(idx3),
    }


def reference(tab_words, tab_scales, dtab_words, dtab_scales, w1, bias, reserve, og, base, offs, offs2, offs3):
    idx = unstriped(offs)
    idx2 = unstriped(offs2)
    idx3 = unstriped(offs3)
    tabu = unpack_weight(tab_words, tab_scales, "e4m3")
    dtabu = unpack_weight(dtab_words, dtab_scales, "e4m3")
    w1q = mxq(f64(w1), 0, "e4m3")
    tabidxg = tabu[:, idx]
    a = w1q.T @ tabidxg
    dtabidxg = dtabu[:, idx]
    ta = w1q.T @ dtabidxg
    h1 = softplus(a + f64(bias))
    s = h1[:, idx2] * h1[:, idx3]
    th1 = ta * sigmoid(a + f64(bias))
    ts = th1[:, idx2] * h1[:, idx3] + th1[:, idx3] * h1[:, idx2]
    tu1 = (ts - (ts + th1[:, idx2]) * s / (s + h1[:, idx2] + f64(reserve))) / (s + h1[:, idx2] + f64(reserve))
    y = tu1 * f64(og) + f64(base)
    return y

@@ -1,0 +1,145 @@
+from contextlib import ExitStack
+
+import concourse.mybir as mybir
+
+K, R, T, J, M = 512, 128, 2048, 512, 256
+FLOPS = 2 * 2 * K * R * J
+
+F32 = mybir.dt.float32
+BF16 = mybir.dt.bfloat16
+I32 = mybir.dt.int32
+U32 = mybir.dt.uint32
+U16 = mybir.dt.uint16
+U8 = mybir.dt.uint8
+FP8X4 = mybir.dt.float8_e4m3fn_x4
+ACT = mybir.ActivationFunctionType
+ALU = mybir.AluOpType
+
+P = 128
+PACK = 4
+HALF = J // 2
+LIST_COLS = HALF // 16
+DTAB_ROW0 = 4
+TINY = 2.0 ** -60
+
+
+def tile_attend_tcpairshare_kernel(tc, tab_words, tab_scales, dtab_words, dtab_scales, w1, bias, reserve, og, base, offs, offs2, offs3, out):
+    nc = tc.nc
+    with ExitStack() as ctx:
+        sb = ctx.enter_context(tc.tile_pool(name="sb", bufs=1))
+        psum = ctx.enter_context(tc.psum_pool(name="psum", bufs=1))
+
+        slots = sb.tile([P, J // 16], U16, name="slots")
+        firsts = sb.tile([P, M // 16], U16, name="firsts")
+        seconds = sb.tile([P, M // 16], U16, name="seconds")
+        tab_s = sb.tile([P, T], U8, name="tab_s", align_bytes=64)
+        dtab_s = sb.tile([P, T], U8, name="dtab_s", align_bytes=64)
+        w_raw = sb.tile([P, PACK, R], F32, name="w_raw", tag="w_then_dtab", align_bytes=64)
+        zero_c = sb.tile([P, 1], F32, name="zero_c", tag="tab_slot", align_bytes=64)
+        tiny_c = sb.tile([P, 1], F32, name="tiny_c")
+        nbias_c = sb.tile([P, 1], F32, name="nbias_c")
+        warm = sb.tile([P, 1], F32, name="warm")
+        bias_c = sb.tile([P, 1], F32, name="bias_c")
+        warm2 = sb.tile([P, 1], F32, name="warm2")
+
+        def words_of(x):
+            return x[0].rearrange("p t b -> p (t b)").bitcast(I32)
+
+        def load_scales(queues, tile, x, row0):
+            rows = x[0].bitcast(I32).rearrange("(q j) c -> j q c", j=4)
+            for j in range(4):
+                queues[j].dma_start(out=tile[row0 + j : P : 32, :].bitcast(I32), in_=rows[j])
+
+        nc.vector.memset(zero_c[:], 0.0)
+        nc.vector.memset(tab_s[:].bitcast(I32), 0)
+        nc.vector.tensor_scalar_add(tiny_c[:], zero_c[:], TINY)
+        nc.vector.memset(dtab_s[:].bitcast(I32), 0)
+
+        nc.sync.dma_start(out=w_raw[:], in_=w1.rearrange("(p j) r -> p j r", j=PACK))
+        nc.sync.dma_start(slots[:], offs)
+        nc.scalar.dma_start(out=bias_c[:], in_=bias)
+        load_scales([nc.sync, nc.scalar, nc.sync, nc.scalar], tab_s, tab_scales, 0)
+        tab_w = sb.tile([P, T], I32, name="tab_w", tag="tab_slot", align_bytes=64)
+        nc.sync.dma_start(out=tab_w[:], in_=words_of(tab_words))
+        load_scales([nc.sync] * 4, dtab_s, dtab_scales, DTAB_ROW0)
+        nc.sync.dma_start(firsts[:], offs2)
+        nc.sync.dma_start(seconds[:], offs3)
+        nc.scalar.activation(warm[:], tiny_c[:], ACT.Sigmoid)
+        nc.scalar.activation(nbias_c[:], bias_c[:], ACT.Copy, scale=-1.0)
+
+        w_neg = sb.tile([P, R, PACK], BF16, name="w_neg", tag="res_slot", align_bytes=64)
+        w_codes = sb.tile([P, R], U32, name="w_codes", align_bytes=64)
+        w_scales = sb.tile([P, R], U8, name="w_scales", align_bytes=64)
+        nc.vector.tensor_scalar_mul(w_neg[:], w_raw[:].rearrange("p j r -> p r j"), -1.0)
+        dtab_w = sb.tile([P, T], I32, name="dtab_w", tag="w_then_dtab", align_bytes=64)
+        nc.sync.dma_start(out=dtab_w[:], in_=words_of(dtab_words))
+        nc.vector.quantize_mx(out=w_codes[:].bitcast(FP8X4), scales=w_scales[:], in_=w_neg[:].rearrange("p r j -> p (r j)"))
+        res_c = sb.tile([P, 1], F32, name="res_c", tag="res_slot", align_bytes=64)
+        nc.sync.dma_start(out=res_c[:], in_=reserve)
+
+        def halves():
+            return [(i, slice(i * HALF, (i + 1) * HALF), slice(i * LIST_COLS, (i + 1) * LIST_COLS)) for i in range(2)]
+
+        def product(words, scales, row0, name, scale_tag, word_tag):
+            g_s = sb.tile([P, J], U8, name=name + "_gs", tag=scale_tag, align_bytes=64)
+            g_w = sb.tile([P, J], U32, name=name + "_gw", tag=word_tag, align_bytes=64)
+            nc.vector.tensor_copy(g_s[:], scales[:].indirect(slots[:]))
+            banks = []
+            for i, cols, lcols in halves():
+                nc.vector.tensor_copy(g_w[:, cols], words[:].bitcast(U32).indirect(slots[:, lcols]))
+                bank = psum.tile([P, HALF], F32, name="%s_bank%d" % (name, i))
+                nc.tensor.matmul_mx(out=bank[:], lhsT=w_codes[:].bitcast(FP8X4), lhsT_scale=w_scales[:],
+                                    rhs=g_w[:, cols].bitcast(FP8X4), rhs_scale=g_s[row0:P, cols], start=True, stop=True)
+                banks.append(bank)
+            return banks
+
+        neg_a = product(tab_w, tab_s, 0, "a", "og_slot", "a_words_then_base")
+        base_t = sb.tile([P, M], F32, name="base_t", tag="a_words_then_base", align_bytes=64)
+        nc.sync.dma_start(out=base_t[:], in_=base)
+        og_c = sb.tile([P, 1], F32, name="og_c", tag="og_slot", align_bytes=64)
+        nc.sync.dma_start(out=og_c[:], in_=og)
+        sig_neg = sb.tile([P, J], F32, name="sig_neg", align_bytes=64)
+        z = sb.tile([P, J], F32, name="z", align_bytes=64)
+        log_sig = sb.tile([P, J], F32, name="log_sig", align_bytes=64)
+        th1 = sb.tile([P, J], F32, name="th1", align_bytes=64)
+        lo, hi = slice(0, HALF), slice(HALF, J)
+        nc.scalar.activation(sig_neg[:, lo], neg_a[0][:], ACT.Sigmoid, bias=nbias_c[:], scale=1.0)
+        nc.scalar.activation(z[:, lo], neg_a[0][:], ACT.Identity, bias=bias_c[:], scale=-1.0)
+        nc.scalar.activation(sig_neg[:, hi], neg_a[1][:], ACT.Sigmoid, bias=nbias_c[:], scale=1.0)
+        nc.scalar.activation(log_sig[:, lo], sig_neg[:, lo], ACT.Ln, bias=tiny_c[:], scale=1.0)
+        nc.scalar.activation(z[:, hi], neg_a[1][:], ACT.Identity, bias=bias_c[:], scale=-1.0)
+        nc.scalar.activation(log_sig[:, hi], sig_neg[:, hi], ACT.Ln, bias=tiny_c[:], scale=1.0)
+        nc.scalar.activation(warm2[:], log_sig[:, J - 1 : J], ACT.Abs_reciprocal_sqrt, bias=1.0, scale=-1.0)
+
+        neg_ta = product(dtab_w, dtab_s, DTAB_ROW0, "ta", "tab_slot", "ta_gw")
+        for i, cols, lcols in halves():
+            nc.vector.scalar_tensor_tensor(th1[:, cols], sig_neg[:, cols], 1.0, neg_ta[i][:], ALU.subtract, ALU.mult)
+        h1 = sb.tile([P, J], F32, name="h1", tag="ta_gw", align_bytes=64)
+        for cols in (lo, hi):
+            nc.vector.scalar_tensor_tensor(h1[:, cols], log_sig[:, cols], -1.0, z[:, cols], ALU.mult, ALU.max)
+
+        def pair_tile(name):
+            return sb.tile([P, M], F32, name=name, align_bytes=64)
+
+        h_a, h_b = pair_tile("h_a"), pair_tile("h_b")
+        nc.vector.tensor_copy(h_a[:], h1[:].indirect(firsts[:]))
+        nc.vector.tensor_copy(h_b[:], h1[:].indirect(seconds[:]))
+        d0, a2 = pair_tile("d0"), pair_tile("a2")
+        nc.vector.scalar_tensor_tensor(a2[:], h_a[:], res_c[:], h_a[:], ALU.add, ALU.mult)
+        nc.vector.scalar_tensor_tensor(d0[:], h_b[:], 1.0, h_a[:], ALU.add, ALU.mult)
+        r1, r2, r4 = pair_tile("r1"), pair_tile("r2"), pair_tile("r4")
+        nc.scalar.activation(r1[:], d0[:], ACT.Abs_reciprocal_sqrt, bias=res_c[:], scale=1.0)
+        nc.scalar.activation(r2[:], r1[:], ACT.Square)
+        nc.scalar.activation(r4[:], r2[:], ACT.Square)
+        term_p, term_q = pair_tile("term_p"), pair_tile("term_q")
+        nc.vector.tensor_tensor(term_q[:], th1[:].indirect(seconds[:]), a2[:], ALU.mult)
+        nc.vector.tensor_tensor(term_p[:], th1[:].indirect(firsts[:]), h_b[:], ALU.mult)
+        num, scaled, y = pair_tile("num"), pair_tile("scaled"), pair_tile("y")
+        pair_halves = [slice(0, M // 2), slice(M // 2, M)]
+        for cols in pair_halves:
+            nc.vector.scalar_tensor_tensor(num[:, cols], term_p[:, cols], res_c[:], term_q[:, cols], ALU.mult, ALU.add)
+        for cols in pair_halves:
+            nc.vector.scalar_tensor_tensor(scaled[:, cols], num[:, cols], og_c[:], r4[:, cols], ALU.mult, ALU.mult)
+        for cols, queue in zip(pair_halves, (nc.sync, nc.scalar)):
+            nc.vector.tensor_tensor(y[:, cols], scaled[:, cols], base_t[:, cols], ALU.add)
+            queue.dma_start(out=out[:, cols], in_=y[:, cols])

@@ -34,8 +34,7 @@ def tile_attend_tcpairshare_kernel(tc, tab_words, tab_scales, dtab_words, dtab_s
         seconds = sb.tile([P, M // 16], U16, name="seconds")
         tab_s = sb.tile([P, T], U8, name="tab_s", align_bytes=64)
         dtab_s = sb.tile([P, T], U8, name="dtab_s", align_bytes=64)
-        w_raw = sb.tile([P, PACK, R], F32, name="w_raw", tag="w_then_dtab", align_bytes=64)
-        zero_c = sb.tile([P, 1], F32, name="zero_c", tag="tab_slot", align_bytes=64)
+        w_raw = sb.tile([P, PACK, R], F32, name="w_raw", align_bytes=64)
         tiny_c = sb.tile([P, 1], F32, name="tiny_c")
         nbias_c = sb.tile([P, 1], F32, name="nbias_c")
         warm = sb.tile([P, 1], F32, name="warm")
@@ -50,9 +49,8 @@ def tile_attend_tcpairshare_kernel(tc, tab_words, tab_scales, dtab_words, dtab_s
             for j in range(4):
                 queues[j].dma_start(out=tile[row0 + j : P : 32, :].bitcast(I32), in_=rows[j])
 
-        nc.vector.memset(zero_c[:], 0.0)
         nc.vector.memset(tab_s[:].bitcast(I32), 0)
-        nc.vector.tensor_scalar_add(tiny_c[:], zero_c[:], TINY)
+        nc.vector.memset(tiny_c[:], TINY)
         nc.vector.memset(dtab_s[:].bitcast(I32), 0)
 
         nc.sync.dma_start(out=w_raw[:], in_=w1.rearrange("(p j) r -> p j r", j=PACK))
@@ -62,6 +60,8 @@ def tile_attend_tcpairshare_kernel(tc, tab_words, tab_scales, dtab_words, dtab_s
         tab_w = sb.tile([P, T], I32, name="tab_w", tag="tab_slot", align_bytes=64)
         nc.sync.dma_start(out=tab_w[:], in_=words_of(tab_words))
         load_scales([nc.sync] * 4, dtab_s, dtab_scales, DTAB_ROW0)
+        dtab_w = sb.tile([P, T], I32, name="dtab_w", align_bytes=64)
+        nc.sync.dma_start(out=dtab_w[:], in_=words_of(dtab_words))
         nc.sync.dma_start(firsts[:], offs2)
         nc.sync.dma_start(seconds[:], offs3)
         nc.scalar.activation(warm[:], tiny_c[:], ACT.Sigmoid)
@@ -71,8 +71,6 @@ def tile_attend_tcpairshare_kernel(tc, tab_words, tab_scales, dtab_words, dtab_s
         w_codes = sb.tile([P, R], U32, name="w_codes", align_bytes=64)
         w_scales = sb.tile([P, R], U8, name="w_scales", align_bytes=64)
         nc.vector.tensor_scalar_mul(w_neg[:], w_raw[:].rearrange("p j r -> p r j"), -1.0)
-        dtab_w = sb.tile([P, T], I32, name="dtab_w", tag="w_then_dtab", align_bytes=64)
-        nc.sync.dma_start(out=dtab_w[:], in_=words_of(dtab_words))
         nc.vector.quantize_mx(out=w_codes[:].bitcast(FP8X4), scales=w_scales[:], in_=w_neg[:].rearrange("p r j -> p (r j)"))
         res_c = sb.tile([P, 1], F32, name="res_c", tag="res_slot", align_bytes=64)
         nc.sync.dma_start(out=res_c[:], in_=reserve)
@@ -80,20 +78,20 @@ def tile_attend_tcpairshare_kernel(tc, tab_words, tab_scales, dtab_words, dtab_s
         def halves():
             return [(i, slice(i * HALF, (i + 1) * HALF), slice(i * LIST_COLS, (i + 1) * LIST_COLS)) for i in range(2)]
 
-        def product(words, scales, row0, name, scale_tag, word_tag):
+        def product(words, scales, row0, name, scale_tag, word_tags):
             g_s = sb.tile([P, J], U8, name=name + "_gs", tag=scale_tag, align_bytes=64)
-            g_w = sb.tile([P, J], U32, name=name + "_gw", tag=word_tag, align_bytes=64)
             nc.vector.tensor_copy(g_s[:], scales[:].indirect(slots[:]))
             banks = []
             for i, cols, lcols in halves():
-                nc.vector.tensor_copy(g_w[:, cols], words[:].bitcast(U32).indirect(slots[:, lcols]))
+                g_w = sb.tile([P, HALF], U32, name="%s_gw%d" % (name, i), tag=word_tags[i], align_bytes=64)
+                nc.vector.tensor_copy(g_w[:], words[:].bitcast(U32).indirect(slots[:, lcols]))
                 bank = psum.tile([P, HALF], F32, name="%s_bank%d" % (name, i))
                 nc.tensor.matmul_mx(out=bank[:], lhsT=w_codes[:].bitcast(FP8X4), lhsT_scale=w_scales[:],
-                                    rhs=g_w[:, cols].bitcast(FP8X4), rhs_scale=g_s[row0:P, cols], start=True, stop=True)
+                                    rhs=g_w[:].bitcast(FP8X4), rhs_scale=g_s[row0:P, cols], start=True, stop=True)
                 banks.append(bank)
             return banks
 
-        neg_a = product(tab_w, tab_s, 0, "a", "og_slot", "a_words_then_base")
+        neg_a = product(tab_w, tab_s, 0, "a", "og_slot", ["a_gw0", "a_words_then_base"])
         base_t = sb.tile([P, M], F32, name="base_t", tag="a_words_then_base", align_bytes=64)
         nc.sync.dma_start(out=base_t[:], in_=base)
         og_c = sb.tile([P, 1], F32, name="og_c", tag="og_slot", align_bytes=64)
@@ -111,11 +109,10 @@ def tile_attend_tcpairshare_kernel(tc, tab_words, tab_scales, dtab_words, dtab_s
         nc.scalar.activation(log_sig[:, hi], sig_neg[:, hi], ACT.Ln, bias=tiny_c[:], scale=1.0)
         nc.scalar.activation(warm2[:], log_sig[:, J - 1 : J], ACT.Abs_reciprocal_sqrt, bias=1.0, scale=-1.0)
 
-        neg_ta = product(dtab_w, dtab_s, DTAB_ROW0, "ta", "tab_slot", "ta_gw")
+        neg_ta = product(dtab_w, dtab_s, DTAB_ROW0, "ta", "tab_slot", ["h1_slot", "ta_gw1"])
+        h1 = sb.tile([P, J], F32, name="h1", tag="h1_slot", align_bytes=64)
         for i, cols, lcols in halves():
             nc.vector.scalar_tensor_tensor(th1[:, cols], sig_neg[:, cols], 1.0, neg_ta[i][:], ALU.subtract, ALU.mult)
-        h1 = sb.tile([P, J], F32, name="h1", tag="ta_gw", align_bytes=64)
-        for cols in (lo, hi):
             nc.vector.scalar_tensor_tensor(h1[:, cols], log_sig[:, cols], -1.0, z[:, cols], ALU.mult, ALU.max)
 
         def pair_tile(name):
@@ -128,14 +125,19 @@ def tile_attend_tcpairshare_kernel(tc, tab_words, tab_scales, dtab_words, dtab_s
         nc.vector.scalar_tensor_tensor(a2[:], h_a[:], res_c[:], h_a[:], ALU.add, ALU.mult)
         nc.vector.scalar_tensor_tensor(d0[:], h_b[:], 1.0, h_a[:], ALU.add, ALU.mult)
         r1, r2, r4 = pair_tile("r1"), pair_tile("r2"), pair_tile("r4")
-        nc.scalar.activation(r1[:], d0[:], ACT.Abs_reciprocal_sqrt, bias=res_c[:], scale=1.0)
-        nc.scalar.activation(r2[:], r1[:], ACT.Square)
-        nc.scalar.activation(r4[:], r2[:], ACT.Square)
-        term_p, term_q = pair_tile("term_p"), pair_tile("term_q")
-        nc.vector.tensor_tensor(term_q[:], th1[:].indirect(seconds[:]), a2[:], ALU.mult)
-        nc.vector.tensor_tensor(term_p[:], th1[:].indirect(firsts[:]), h_b[:], ALU.mult)
-        num, scaled, y = pair_tile("num"), pair_tile("scaled"), pair_tile("y")
         pair_halves = [slice(0, M // 2), slice(M // 2, M)]
+        list_halves = [slice(0, M // 32), slice(M // 32, M // 16)]
+        for cols in pair_halves:
+            nc.scalar.activation(r1[:, cols], d0[:, cols], ACT.Abs_reciprocal_sqrt, bias=res_c[:], scale=1.0)
+        for cols in pair_halves:
+            nc.scalar.activation(r2[:, cols], r1[:, cols], ACT.Square)
+        for cols in pair_halves:
+            nc.scalar.activation(r4[:, cols], r2[:, cols], ACT.Square)
+        term_p, term_q = pair_tile("term_p"), pair_tile("term_q")
+        for cols, lcols in zip(pair_halves, list_halves):
+            nc.vector.tensor_tensor(term_q[:, cols], th1[:].indirect(seconds[:, lcols]), a2[:, cols], ALU.mult)
+            nc.vector.tensor_tensor(term_p[:, cols], th1[:].indirect(firsts[:, lcols]), h_b[:, cols], ALU.mult)
+        num, scaled, y = pair_tile("num"), pair_tile("scaled"), pair_tile("y")
         for cols in pair_halves:
             nc.vector.scalar_tensor_tensor(num[:, cols], term_p[:, cols], res_c[:], term_q[:, cols], ALU.mult, ALU.add)
         for cols in pair_halves:

from contextlib import ExitStack

import concourse.mybir as mybir

K, R, T, J, M = 512, 128, 2048, 512, 256
FLOPS = 2 * 2 * K * R * J

F32 = mybir.dt.float32
BF16 = mybir.dt.bfloat16
I32 = mybir.dt.int32
U32 = mybir.dt.uint32
U16 = mybir.dt.uint16
U8 = mybir.dt.uint8
FP8X4 = mybir.dt.float8_e4m3fn_x4
ACT = mybir.ActivationFunctionType
ALU = mybir.AluOpType

P = 128
PACK = 4
HALF = J // 2
LIST_COLS = HALF // 16
DTAB_ROW0 = 4
TINY = 2.0 ** -60


def tile_attend_tcpairshare_kernel(tc, tab_words, tab_scales, dtab_words, dtab_scales, w1, bias, reserve, og, base, offs, offs2, offs3, out):
    nc = tc.nc
    with ExitStack() as ctx:
        sb = ctx.enter_context(tc.tile_pool(name="sb", bufs=1))
        psum = ctx.enter_context(tc.psum_pool(name="psum", bufs=1))

        slots = sb.tile([P, J // 16], U16, name="slots")
        firsts = sb.tile([P, M // 16], U16, name="firsts")
        seconds = sb.tile([P, M // 16], U16, name="seconds")
        tab_s = sb.tile([P, T], U8, name="tab_s", align_bytes=64)
        dtab_s = sb.tile([P, T], U8, name="dtab_s", align_bytes=64)
        w_raw = sb.tile([P, PACK, R], F32, name="w_raw", align_bytes=64)
        tiny_c = sb.tile([P, 1], F32, name="tiny_c")
        nbias_c = sb.tile([P, 1], F32, name="nbias_c")
        warm = sb.tile([P, 1], F32, name="warm")
        bias_c = sb.tile([P, 1], F32, name="bias_c")
        warm2 = sb.tile([P, 1], F32, name="warm2")

        def words_of(x):
            return x[0].rearrange("p t b -> p (t b)").bitcast(I32)

        def load_scales(queues, tile, x, row0):
            rows = x[0].bitcast(I32).rearrange("(q j) c -> j q c", j=4)
            for j in range(4):
                queues[j].dma_start(out=tile[row0 + j : P : 32, :].bitcast(I32), in_=rows[j])

        nc.vector.memset(tab_s[:].bitcast(I32), 0)
        nc.vector.memset(tiny_c[:], TINY)
        nc.vector.memset(dtab_s[:].bitcast(I32), 0)

        nc.sync.dma_start(out=w_raw[:], in_=w1.rearrange("(p j) r -> p j r", j=PACK))
        nc.sync.dma_start(slots[:], offs)
        nc.scalar.dma_start(out=bias_c[:], in_=bias)
        load_scales([nc.sync, nc.scalar, nc.sync, nc.scalar], tab_s, tab_scales, 0)
        tab_w = sb.tile([P, T], I32, name="tab_w", tag="tab_slot", align_bytes=64)
        nc.sync.dma_start(out=tab_w[:], in_=words_of(tab_words))
        load_scales([nc.sync] * 4, dtab_s, dtab_scales, DTAB_ROW0)
        dtab_w = sb.tile([P, T], I32, name="dtab_w", align_bytes=64)
        nc.sync.dma_start(out=dtab_w[:], in_=words_of(dtab_words))
        nc.sync.dma_start(firsts[:], offs2)
        nc.sync.dma_start(seconds[:], offs3)
        nc.scalar.activation(warm[:], tiny_c[:], ACT.Sigmoid)
        nc.scalar.activation(nbias_c[:], bias_c[:], ACT.Copy, scale=-1.0)

        w_neg = sb.tile([P, R, PACK], BF16, name="w_neg", tag="res_slot", align_bytes=64)
        w_codes = sb.tile([P, R], U32, name="w_codes", align_bytes=64)
        w_scales = sb.tile([P, R], U8, name="w_scales", align_bytes=64)
        nc.vector.tensor_scalar_mul(w_neg[:], w_raw[:].rearrange("p j r -> p r j"), -1.0)
        nc.vector.quantize_mx(out=w_codes[:].bitcast(FP8X4), scales=w_scales[:], in_=w_neg[:].rearrange("p r j -> p (r j)"))
        res_c = sb.tile([P, 1], F32, name="res_c", tag="res_slot", align_bytes=64)
        nc.sync.dma_start(out=res_c[:], in_=reserve)

        def halves():
            return [(i, slice(i * HALF, (i + 1) * HALF), slice(i * LIST_COLS, (i + 1) * LIST_COLS)) for i in range(2)]

        def product(words, scales, row0, name, scale_tag, word_tags):
            g_s = sb.tile([P, J], U8, name=name + "_gs", tag=scale_tag, align_bytes=64)
            nc.vector.tensor_copy(g_s[:], scales[:].indirect(slots[:]))
            banks = []
            for i, cols, lcols in halves():
                g_w = sb.tile([P, HALF], U32, name="%s_gw%d" % (name, i), tag=word_tags[i], align_bytes=64)
                nc.vector.tensor_copy(g_w[:], words[:].bitcast(U32).indirect(slots[:, lcols]))
                bank = psum.tile([P, HALF], F32, name="%s_bank%d" % (name, i))
                nc.tensor.matmul_mx(out=bank[:], lhsT=w_codes[:].bitcast(FP8X4), lhsT_scale=w_scales[:],
                                    rhs=g_w[:].bitcast(FP8X4), rhs_scale=g_s[row0:P, cols], start=True, stop=True)
                banks.append(bank)
            return banks

        neg_a = product(tab_w, tab_s, 0, "a", "og_slot", ["a_gw0", "a_words_then_base"])
        base_t = sb.tile([P, M], F32, name="base_t", tag="a_words_then_base", align_bytes=64)
        nc.sync.dma_start(out=base_t[:], in_=base)
        og_c = sb.tile([P, 1], F32, name="og_c", tag="og_slot", align_bytes=64)
        nc.sync.dma_start(out=og_c[:], in_=og)
        sig_neg = sb.tile([P, J], F32, name="sig_neg", align_bytes=64)
        z = sb.tile([P, J], F32, name="z", align_bytes=64)
        log_sig = sb.tile([P, J], F32, name="log_sig", align_bytes=64)
        th1 = sb.tile([P, J], F32, name="th1", align_bytes=64)
        lo, hi = slice(0, HALF), slice(HALF, J)
        nc.scalar.activation(sig_neg[:, lo], neg_a[0][:], ACT.Sigmoid, bias=nbias_c[:], scale=1.0)
        nc.scalar.activation(z[:, lo], neg_a[0][:], ACT.Identity, bias=bias_c[:], scale=-1.0)
        nc.scalar.activation(sig_neg[:, hi], neg_a[1][:], ACT.Sigmoid, bias=nbias_c[:], scale=1.0)
        nc.scalar.activation(log_sig[:, lo], sig_neg[:, lo], ACT.Ln, bias=tiny_c[:], scale=1.0)
        nc.scalar.activation(z[:, hi], neg_a[1][:], ACT.Identity, bias=bias_c[:], scale=-1.0)
        nc.scalar.activation(log_sig[:, hi], sig_neg[:, hi], ACT.Ln, bias=tiny_c[:], scale=1.0)
        nc.scalar.activation(warm2[:], log_sig[:, J - 1 : J], ACT.Abs_reciprocal_sqrt, bias=1.0, scale=-1.0)

        neg_ta = product(dtab_w, dtab_s, DTAB_ROW0, "ta", "tab_slot", ["h1_slot", "ta_gw1"])
        h1 = sb.tile([P, J], F32, name="h1", tag="h1_slot", align_bytes=64)
        for i, cols, lcols in halves():
            nc.vector.scalar_tensor_tensor(th1[:, cols], sig_neg[:, cols], 1.0, neg_ta[i][:], ALU.subtract, ALU.mult)
            nc.vector.scalar_tensor_tensor(h1[:, cols], log_sig[:, cols], -1.0, z[:, cols], ALU.mult, ALU.max)

        def pair_tile(name):
            return sb.tile([P, M], F32, name=name, align_bytes=64)

        h_a, h_b = pair_tile("h_a"), pair_tile("h_b")
        nc.vector.tensor_copy(h_a[:], h1[:].indirect(firsts[:]))
        nc.vector.tensor_copy(h_b[:], h1[:].indirect(seconds[:]))
        d0, a2 = pair_tile("d0"), pair_tile("a2")
        nc.vector.scalar_tensor_tensor(a2[:], h_a[:], res_c[:], h_a[:], ALU.add, ALU.mult)
        nc.vector.scalar_tensor_tensor(d0[:], h_b[:], 1.0, h_a[:], ALU.add, ALU.mult)
        r1, r2, r4 = pair_tile("r1"), pair_tile("r2"), pair_tile("r4")
        pair_halves = [slice(0, M // 2), slice(M // 2, M)]
        list_halves = [slice(0, M // 32), slice(M // 32, M // 16)]
        for cols in pair_halves:
            nc.scalar.activation(r1[:, cols], d0[:, cols], ACT.Abs_reciprocal_sqrt, bias=res_c[:], scale=1.0)
        for cols in pair_halves:
            nc.scalar.activation(r2[:, cols], r1[:, cols], ACT.Square)
        for cols in pair_halves:
            nc.scalar.activation(r4[:, cols], r2[:, cols], ACT.Square)
        term_p, term_q = pair_tile("term_p"), pair_tile("term_q")
        for cols, lcols in zip(pair_halves, list_halves):
            nc.vector.tensor_tensor(term_q[:, cols], th1[:].indirect(seconds[:, lcols]), a2[:, cols], ALU.mult)
            nc.vector.tensor_tensor(term_p[:, cols], th1[:].indirect(firsts[:, lcols]), h_b[:, cols], ALU.mult)
        num, scaled, y = pair_tile("num"), pair_tile("scaled"), pair_tile("y")
        for cols in pair_halves:
            nc.vector.scalar_tensor_tensor(num[:, cols], term_p[:, cols], res_c[:], term_q[:, cols], ALU.mult, ALU.add)
        for cols in pair_halves:
            nc.vector.scalar_tensor_tensor(scaled[:, cols], num[:, cols], og_c[:], r4[:, cols], ALU.mult, ALU.mult)
        for cols, queue in zip(pair_halves, (nc.sync, nc.scalar)):
            nc.vector.tensor_tensor(y[:, cols], scaled[:, cols], base_t[:, cols], ALU.add)
            queue.dma_start(out=out[:, cols], in_=y[:, cols])
